import numpy as np
import ml_dtypes


def mxq(x, axis, fmt="e4m3"):
    dtype, down = {"e4m3": (ml_dtypes.float8_e4m3fn, 7), "e5m2": (ml_dtypes.float8_e5m2, 14)}[fmt]
    v = np.moveaxis(np.asarray(x, np.float32).astype(ml_dtypes.bfloat16).astype(np.float64), axis, -1)
    blocks = v.reshape(v.shape[:-1] + (-1, 32))
    amax = np.abs(blocks).max(-1, keepdims=True)
    byte = np.maximum(np.where(amax > 0, np.frexp(amax)[1] - 1 + 127, 0) - down, 1)
    scale = np.exp2(byte - 127.0)
    codes = (blocks / scale).astype(np.float32).astype(dtype).astype(np.float64)
    return np.moveaxis((codes * scale).reshape(v.shape), -1, axis)


WIDE = False


def mx_kscale(k):
    if not WIDE:
        return np.ones(k)
    levels = np.array([10, -10, 5, -5, 0])
    if k % 512:
        return np.exp2(np.random.permutation(np.resize(levels, k // 32))).repeat(32)
    a = np.empty((k // 512, 16))
    for p in range(k // 512):
        a[p, :8] = np.random.permutation(np.resize(levels, 8))
        for g in range(8):
            far = levels[np.abs(levels - a[p, g]) >= 10]
            a[p, g + 8] = far[np.random.randint(len(far))]
    return np.exp2(a.ravel()).repeat(32)


def f64(x):
    return np.asarray(x).astype(np.float64)


def striped(idx):
    return np.tile(idx.reshape(-1, 16).T, (8, 1)).astype(np.uint16)


def unstriped(offs):
    return offs[:16].T.reshape(-1).astype(np.int64)


def striped8(idx):
    return np.concatenate([x.reshape(-1, 16).T for x in idx]).astype(np.uint16)


def runs(offs, k):
    lists = np.stack([offs[16 * r : 16 * r + 16].T.reshape(-1) for r in range(8)]).astype(np.int64)
    return lists[np.arange(k) % 512 // 64]


def pack_weight(w):
    k, n = w.shape
    w = f64(np.asarray(w, np.float32).astype(ml_dtypes.bfloat16)).reshape(k // 32, 32, n)
    amax = np.abs(w).max(1)
    byte = np.clip(np.where(amax > 0, np.frexp(amax)[1] - 1 + 127 - 7, 1), 1, 254)
    scaled = (w * np.exp2(127.0 - byte)[:, None, :]).reshape(k, n).astype(np.float32)
    words = np.ascontiguousarray(scaled.reshape(k // 512, 128, 4, n).transpose(0, 1, 3, 2)).astype(ml_dtypes.float8_e4m3fn).view(np.uint8)
    return words, np.ascontiguousarray(byte.astype(np.uint8).reshape(k // 512, 16, n))


def unpack_weight(words, scales):
    g, p, n, _ = words.shape
    vals = np.ascontiguousarray(words).view(ml_dtypes.float8_e4m3fn).astype(np.float64) * np.repeat(np.exp2(scales.astype(np.float64) - 127.0), 8, axis=1)[..., None]
    return vals.transpose(0, 1, 3, 2).reshape(g * 512, n)


E2M1 = np.array([0.0, 0.5, 1.0, 1.5, 2.0, 3.0, 4.0, 6.0, -0.0, -0.5, -1.0, -1.5, -2.0, -3.0, -4.0, -6.0])


def pack_fp4(w):
    k, n = w.shape
    w = f64(np.asarray(w, np.float32).astype(ml_dtypes.bfloat16)).reshape(k // 32, 32, n)
    amax = np.abs(w).max(1)
    mant, ex = np.frexp(amax / 6.0)
    byte = np.clip(np.where(amax > 0, np.where(mant > 0.5, ex, ex - 1) + 127, 1), 1, 254)
    scaled = (w * np.exp2(127.0 - byte)[:, None, :]).reshape(k, n).astype(np.float32)
    c = np.ascontiguousarray(scaled.reshape(k // 512, 128, 4, n).transpose(0, 1, 3, 2)).astype(ml_dtypes.float4_e2m1fn).view(np.uint8) & 0xF
    words = (c[..., 0::2] | (c[..., 1::2] << 4)).reshape(k // 512, 128, 2 * n)
    return np.ascontiguousarray(words), np.ascontiguousarray(byte.astype(np.uint8).reshape(k // 512, 16, n))


def unpack_fp4(words, scales):
    g, _, n = scales.shape
    words = np.ascontiguousarray(words).reshape(g, 128, n, 2)
    nib = np.empty((g, 128, n, 4), np.uint8)
    nib[..., 0::2] = words & 0xF
    nib[..., 1::2] = words >> 4
    vals = E2M1[nib] * np.repeat(np.exp2(scales.astype(np.float64) - 127.0), 8, axis=1)[..., None]
    return vals.transpose(0, 1, 3, 2).reshape(g * 512, n)


def sigmoid(v):
    return 1.0 / (1.0 + np.exp(-np.maximum(v, -700.0)))

def planes(y):
    n, m = y.shape
    v = y.astype(np.float32).astype(ml_dtypes.bfloat16).astype(np.float64).reshape(n // 32, 32, m)
    top = np.abs(v).max(1)
    byte = np.clip(np.where(top > 0, np.frexp(top)[1] - 1 + 127 - 7, 1), 1, 254)
    codes = (v * np.exp2(127.0 - byte)[:, None, :]).reshape(n, m).astype(np.float32).astype(ml_dtypes.float8_e4m3fn).view(np.uint8)
    words = codes.reshape(n // 512, 128, 4, m).transpose(0, 1, 3, 2)
    return np.ascontiguousarray(words), np.ascontiguousarray(byte.astype(np.uint8).reshape(n // 512, 16, m))


K, T, S, V, N, H = 512, 2048, 512, 256, 512, 512


def setup_inputs():
    n = np.random.standard_normal
    s = mx_kscale(K)[:, None]
    u = mx_kscale(S)
    packed_xT = pack_weight(n((K, T)) * s)
    packed_w1 = pack_fp4(n((S, N)) / np.sqrt(S) / u[:, None])
    return {
        "x_words": packed_xT[0],
        "x_scales": packed_xT[1],
        "wa": (n((K, H)) / np.sqrt(K) / s).astype(np.float32),
        "gt": (np.random.uniform(0.5, 1.5, (S, 1)) * u[:, None]).astype(np.float32),
        "w1_words": packed_w1[0],
        "w1_scales": packed_w1[1],
        "offs": striped(np.random.permutation(T)[:S]),
        "fa": striped8(np.stack([np.random.permutation(H)[:V] for _ in range(8)])),
        "fb": striped8(np.stack([np.random.permutation(H)[:V] for _ in range(8)])),
    }


def reference(x_words, x_scales, wa, gt, w1_words, w1_scales, offs, fa, fb):
    xq = unpack_weight(x_words, x_scales)[:, unstriped(offs)]
    y = xq.T @ mxq(f64(wa), 0, "e4m3")
    z = f64(gt) * ((y[np.arange(S)[:, None], runs(fa, S)]) * (sigmoid(y[np.arange(S)[:, None], runs(fb, S)])))
    out_0 = unpack_fp4(w1_words, w1_scales).T @ mxq(z, 0, "e4m3")
    return (out_0,) + planes(out_0)

@@ -1,0 +1,149 @@
+from contextlib import ExitStack
+
+import concourse.mybir as mybir
+
+K, T, S, V, N, H = 512, 2048, 512, 256, 512, 512
+FLOPS = 2 * S * K * H + 2 * N * S * V
+
+F32 = mybir.dt.float32
+BF16 = mybir.dt.bfloat16
+I32 = mybir.dt.int32
+U32 = mybir.dt.uint32
+U16 = mybir.dt.uint16
+U8 = mybir.dt.uint8
+FP8X4 = mybir.dt.float8_e4m3fn_x4
+FP4X4 = mybir.dt.float4_e2m1fn_x4
+MULT = mybir.AluOpType.mult
+SIGMOID = mybir.ActivationFunctionType.Sigmoid
+
+P = 128
+PACK = 4
+HH = H // 2
+VH = V // 2
+VEC_COLS = 176
+
+
+def weave(ap_out, ap_in):
+    return (
+        ap_out.rearrange("p (c i) t -> p c t i", i=PACK),
+        ap_in.rearrange("p t (c i) -> p c t i", i=PACK),
+    )
+
+
+def tile_picked_featglu_none_po_kernel(tc, x_words, x_scales, wa, gt, w1_words, w1_scales, offs, fa, fb, out_0, out_1, out_2):
+    nc = tc.nc
+    with ExitStack() as ctx:
+        keep = ctx.enter_context(tc.tile_pool(name="keep", bufs=1))
+        psum = ctx.enter_context(tc.psum_pool(name="psum", bufs=1))
+
+        offs_t = keep.tile([P, S // 16], U16, name="offs_t")
+        fa_t = keep.tile([P, V // 16], U16, name="fa_t")
+        fb_t = keep.tile([P, V // 16], U16, name="fb_t")
+        xw_all = keep.tile([P, T], I32, name="xw_all", align_bytes=64)
+        xs_all = keep.tile([P, T], U8, name="xs_all", align_bytes=64)
+        wa_raw = [keep.tile([P, PACK, HH], F32, name=f"wa_raw{h}", align_bytes=64) for h in range(2)]
+        gate = keep.tile([P, PACK], F32, name="gate")
+        w1w_raw = keep.tile([P, 2 * N], U8, name="w1w_raw", align_bytes=64)
+        w1s_raw = keep.tile([P, N], U8, name="w1s_raw", align_bytes=64)
+        warm_in = keep.tile([P, 1], F32, name="warm_in")
+        warm_out = keep.tile([P, 1], F32, name="warm_out")
+
+        nc.vector.memset(warm_in[:], 0.0)
+        nc.vector.memset(xs_all[:].bitcast(I32), 0)
+        nc.vector.memset(w1s_raw[:].bitcast(I32), 0)
+
+        wa_v = wa.rearrange("(p j) c -> p j c", j=PACK)
+        nc.sync.dma_start(offs_t[:], offs)
+        nc.sync.dma_start(fa_t[:], fa)
+        nc.sync.dma_start(wa_raw[0][:], wa_v[:, :, 0:HH])
+        nc.sync.dma_start(xw_all[:], x_words[0].rearrange("p n r -> p (n r)").bitcast(I32))
+        nc.sync.dma_start(wa_raw[1][:], wa_v[:, :, HH:H])
+        nc.sync.dma_start(fb_t[:], fb)
+        nc.scalar.dma_start(w1w_raw[:].bitcast(I32), w1_words[0].bitcast(I32))
+        nc.scalar.dma_start(gate[:], gt.rearrange("(p t) o -> p (t o)", t=PACK))
+        nc.scalar.activation(warm_out[:], warm_in[:], SIGMOID)
+        for q in range(4):
+            nc.scalar.dma_start(xs_all[32 * q : 32 * q + 4, :].bitcast(I32), x_scales[0][4 * q : 4 * q + 4, :].bitcast(I32))
+        for q in range(4):
+            nc.sync.dma_start(w1s_raw[32 * q : 32 * q + 4, :].bitcast(I32), w1_scales[0][4 * q : 4 * q + 4, :].bitcast(I32))
+
+        wa_bf = [keep.tile([P, HH, PACK], BF16, name=f"wa_bf{h}", align_bytes=64) for h in range(2)]
+        wa_q = [keep.tile([P, HH], U32, name=f"wa_q{h}", align_bytes=64) for h in range(2)]
+        wa_s = [keep.tile([P, HH], U8, name=f"wa_s{h}", align_bytes=64) for h in range(2)]
+        w1w = keep.tile([P, PACK, 2 * P], U8, name="w1w", align_bytes=64)
+        w1s = keep.tile([P, PACK, P], U8, name="w1s", align_bytes=64)
+        xs_pick = keep.tile([P, S], U8, name="xs_pick", align_bytes=64)
+        xs = keep.tile([P, PACK, P], U8, name="xs", align_bytes=64)
+        xw = keep.tile([P, PACK, P], U32, name="xw", align_bytes=64)
+
+        nc.scalar.copy(*weave(wa_bf[0][:], wa_raw[0][:]))
+        nc.vector.tensor_copy(
+            w1w[:].rearrange("p t (m b) -> p m t b", b=2), w1w_raw[:].rearrange("p (m t b) -> p m t b", t=PACK, b=2)
+        )
+        nc.vector.tensor_copy(xs_pick[:], xs_all[:].indirect(offs_t[:]))
+        nc.vector.quantize_mx(wa_q[0][:].bitcast(FP8X4), wa_s[0][:], wa_bf[0][:].rearrange("p c j -> p (c j)"))
+        nc.vector.tensor_copy(xs[:].rearrange("p t m -> p m t"), xs_pick[:].rearrange("p (m t) -> p m t", t=PACK))
+        nc.vector.tensor_copy(xw[:].rearrange("p t m -> p m t"), xw_all[:].bitcast(U32).indirect(offs_t[:]))
+
+        nc.vector.tensor_copy(*weave(wa_bf[1][:, 0:VEC_COLS, :], wa_raw[1][:, :, 0:VEC_COLS]))
+        nc.scalar.copy(*weave(wa_bf[1][:, VEC_COLS:HH, :], wa_raw[1][:, :, VEC_COLS:HH]))
+        nc.vector.quantize_mx(wa_q[1][:].bitcast(FP8X4), wa_s[1][:], wa_bf[1][:].rearrange("p c j -> p (c j)"))
+
+        y = [keep.tile([P, H], F32, name=f"y{t}", align_bytes=64) for t in range(PACK)]
+        for h in range(2):
+            for t in range(PACK):
+                acc = psum.tile([P, HH], F32, name=f"acc{t}{h}", tag=f"bank{t}{h}")
+                nc.tensor.matmul_mx(
+                    acc[:], lhsT=xw[:, t, :].bitcast(FP8X4), lhsT_scale=xs[:, t, :],
+                    rhs=wa_q[h][:].bitcast(FP8X4), rhs_scale=wa_s[h][:], start=True, stop=True,
+                )
+                if h == 1 and t > 0:
+                    nc.vector.tensor_copy(y[t][:, h * HH : (h + 1) * HH], acc[:])
+                else:
+                    nc.scalar.copy(y[t][:, h * HH : (h + 1) * HH], acc[:])
+
+        nc.vector.tensor_copy(w1s[:].rearrange("p t m -> p m t"), w1s_raw[:].rearrange("p (m t) -> p m t", t=PACK))
+
+        out_v = out_0.rearrange("(p t) v -> p t v", t=PACK)
+        words_v = out_1[0].rearrange("p n r -> p (n r)").bitcast(I32)
+        o_q = keep.tile([P, V], U32, name="o_q", align_bytes=64)
+        o_s = keep.tile([P, V], U8, name="o_s", align_bytes=64)
+        z_q, z_s = [], []
+        for g in range(2):
+            cols = slice(g * VH // 16, (g + 1) * VH // 16)
+            zf = keep.tile([P, PACK, VH], F32, name=f"zf{g}", align_bytes=64)
+            for t in range(PACK):
+                sg = keep.tile([P, VH], F32, name=f"sg{g}{t}", align_bytes=64)
+                nc.scalar.activation(sg[:], y[t][:].indirect(fb_t[:, cols]), SIGMOID)
+                nc.vector.tensor_tensor(zf[:, t, :], y[t][:].indirect(fa_t[:, cols]), sg[:], MULT)
+            zb = keep.tile([P, VH, PACK], BF16, name=f"zb{g}", align_bytes=64)
+            zo, zi = weave(zb[:], zf[:])
+            nc.vector.tensor_tensor(
+                zo, zi, gate[:].rearrange("p (c t i) -> p c t i", c=1, i=1).to_broadcast([P, VH // PACK, PACK, PACK]), MULT
+            )
+            z_q.append(keep.tile([P, VH], U32, name=f"z_q{g}", align_bytes=64))
+            z_s.append(keep.tile([P, VH], U8, name=f"z_s{g}", align_bytes=64))
+            nc.vector.quantize_mx(z_q[g][:].bitcast(FP8X4), z_s[g][:], zb[:].rearrange("p v t -> p (v t)"))
+
+        for g in range(2):
+            vs = slice(g * VH, (g + 1) * VH)
+            acc = psum.tile([P, PACK, VH], F32, name=f"res{g}", tag=f"bank{g}0")
+            for t in range(PACK):
+                nc.tensor.matmul_mx(
+                    acc[:, t, :], lhsT=w1w[:, t, :].bitcast(FP4X4), lhsT_scale=w1s[:, t, :],
+                    rhs=z_q[g][:].bitcast(FP8X4), rhs_scale=z_s[g][:], start=True, stop=True,
+                )
+            of = keep.tile([P, PACK, VH], F32, name=f"of{g}", align_bytes=64)
+            ob = keep.tile([P, VH, PACK], BF16, name=f"ob{g}", align_bytes=64)
+            if g == 0:
+                nc.scalar.copy(of[:], acc[:])
+                nc.vector.tensor_copy(*weave(ob[:], of[:]))
+            else:
+                nc.vector.tensor_copy(ob[:], acc[:].rearrange("p t v -> p v t"))
+                nc.scalar.copy(of[:], acc[:])
+            nc.sync.dma_start(out_v[:, :, vs], of[:])
+            nc.vector.quantize_mx(o_q[:, vs].bitcast(FP8X4), o_s[:, vs], ob[:].rearrange("p v t -> p (v t)"))
+            nc.sync.dma_start(words_v[:, vs], o_q[:, vs].bitcast(I32))
+        for q in range(4):
+            eng = nc.sync if q % 2 == 0 else nc.scalar
+            eng.dma_start(out_2[0][4 * q : 4 * q + 4, :].bitcast(I32), o_s[32 * q : 32 * q + 4, :].bitcast(I32))

@@ -14,6 +14,7 @@ U8 = mybir.dt.uint8
 FP8X4 = mybir.dt.float8_e4m3fn_x4
 FP4X4 = mybir.dt.float4_e2m1fn_x4
 MULT = mybir.AluOpType.mult
+COPY = mybir.ActivationFunctionType.Copy
 SIGMOID = mybir.ActivationFunctionType.Sigmoid
 
 P = 128
@@ -34,62 +35,66 @@ def tile_picked_featglu_none_po_kernel(tc, x_words, x_scales, wa, gt, w1_words, 
     nc = tc.nc
     with ExitStack() as ctx:
         keep = ctx.enter_context(tc.tile_pool(name="keep", bufs=1))
+        stage = ctx.enter_context(tc.tile_pool(name="stage", bufs=1))
         psum = ctx.enter_context(tc.psum_pool(name="psum", bufs=1))
 
         offs_t = keep.tile([P, S // 16], U16, name="offs_t")
         fa_t = keep.tile([P, V // 16], U16, name="fa_t")
         fb_t = keep.tile([P, V // 16], U16, name="fb_t")
-        xw_all = keep.tile([P, T], I32, name="xw_all", align_bytes=64)
-        xs_all = keep.tile([P, T], U8, name="xs_all", align_bytes=64)
-        wa_raw = [keep.tile([P, PACK, HH], F32, name=f"wa_raw{h}", align_bytes=64) for h in range(2)]
+        xw_all = keep.tile([P, T], I32, name="xw_all", tag="late", align_bytes=64)
+        xs_all = keep.tile([P, T], U8, name="xs_all", tag="mid", align_bytes=64)
+        wa_both = stage.tile([P, 2, PACK, HH], F32, name="wa_both", offset=0)
+        wa_raw = [wa_both[:, h] for h in range(2)]
         gate = keep.tile([P, PACK], F32, name="gate")
         w1w_raw = keep.tile([P, 2 * N], U8, name="w1w_raw", align_bytes=64)
         w1s_raw = keep.tile([P, N], U8, name="w1s_raw", align_bytes=64)
         warm_in = keep.tile([P, 1], F32, name="warm_in")
         warm_out = keep.tile([P, 1], F32, name="warm_out")
 
-        nc.vector.memset(warm_in[:], 0.0)
         nc.vector.memset(xs_all[:].bitcast(I32), 0)
+        nc.vector.memset(warm_in[:], 0.0)
         nc.vector.memset(w1s_raw[:].bitcast(I32), 0)
 
         wa_v = wa.rearrange("(p j) c -> p j c", j=PACK)
         nc.sync.dma_start(offs_t[:], offs)
-        nc.sync.dma_start(fa_t[:], fa)
-        nc.sync.dma_start(wa_raw[0][:], wa_v[:, :, 0:HH])
-        nc.sync.dma_start(xw_all[:], x_words[0].rearrange("p n r -> p (n r)").bitcast(I32))
-        nc.sync.dma_start(wa_raw[1][:], wa_v[:, :, HH:H])
-        nc.sync.dma_start(fb_t[:], fb)
-        nc.scalar.dma_start(w1w_raw[:].bitcast(I32), w1_words[0].bitcast(I32))
-        nc.scalar.dma_start(gate[:], gt.rearrange("(p t) o -> p (t o)", t=PACK))
-        nc.scalar.activation(warm_out[:], warm_in[:], SIGMOID)
+        nc.sync.dma_start(w1w_raw[:].bitcast(I32), w1_words[0].bitcast(I32))
+        nc.sync.dma_start(wa_raw[0], wa_v[:, :, 0:HH])
         for q in range(4):
-            nc.scalar.dma_start(xs_all[32 * q : 32 * q + 4, :].bitcast(I32), x_scales[0][4 * q : 4 * q + 4, :].bitcast(I32))
+            nc.sync.dma_start(xs_all[32 * q : 32 * q + 4, :].bitcast(I32), x_scales[0][4 * q : 4 * q + 4, :].bitcast(I32))
+        nc.sync.dma_start(xw_all[:], x_words[0].rearrange("p n r -> p (n r)").bitcast(I32))
+        nc.sync.dma_start(wa_raw[1], wa_v[:, :, HH:H])
         for q in range(4):
             nc.sync.dma_start(w1s_raw[32 * q : 32 * q + 4, :].bitcast(I32), w1_scales[0][4 * q : 4 * q + 4, :].bitcast(I32))
+        nc.sync.dma_start(fb_t[:], fb)
+        nc.sync.dma_start(fa_t[:], fa)
+        nc.sync.dma_start(gate[:], gt.rearrange("(p t) o -> p (t o)", t=PACK))
+        nc.scalar.activation(warm_out[:], warm_in[:], SIGMOID)
 
-        wa_bf = [keep.tile([P, HH, PACK], BF16, name=f"wa_bf{h}", align_bytes=64) for h in range(2)]
-        wa_q = [keep.tile([P, HH], U32, name=f"wa_q{h}", align_bytes=64) for h in range(2)]
+        wa_bf = [keep.tile([P, HH, PACK], BF16, name="wa_bf0", align_bytes=64)]
         wa_s = [keep.tile([P, HH], U8, name=f"wa_s{h}", align_bytes=64) for h in range(2)]
         w1w = keep.tile([P, PACK, 2 * P], U8, name="w1w", align_bytes=64)
-        w1s = keep.tile([P, PACK, P], U8, name="w1s", align_bytes=64)
         xs_pick = keep.tile([P, S], U8, name="xs_pick", align_bytes=64)
         xs = keep.tile([P, PACK, P], U8, name="xs", align_bytes=64)
         xw = keep.tile([P, PACK, P], U32, name="xw", align_bytes=64)
 
-        nc.scalar.copy(*weave(wa_bf[0][:], wa_raw[0][:]))
+        nc.scalar.copy(*weave(wa_bf[0][:], wa_raw[0]))
         nc.vector.tensor_copy(
             w1w[:].rearrange("p t (m b) -> p m t b", b=2), w1w_raw[:].rearrange("p (m t b) -> p m t b", t=PACK, b=2)
         )
         nc.vector.tensor_copy(xs_pick[:], xs_all[:].indirect(offs_t[:]))
+        wa_q = [keep.tile([P, HH], U32, name="wa_q0", tag="mid", align_bytes=64), keep.tile([P, HH], U32, name="wa_q1", align_bytes=64)]
         nc.vector.quantize_mx(wa_q[0][:].bitcast(FP8X4), wa_s[0][:], wa_bf[0][:].rearrange("p c j -> p (c j)"))
         nc.vector.tensor_copy(xs[:].rearrange("p t m -> p m t"), xs_pick[:].rearrange("p (m t) -> p m t", t=PACK))
         nc.vector.tensor_copy(xw[:].rearrange("p t m -> p m t"), xw_all[:].bitcast(U32).indirect(offs_t[:]))
 
+        wa_bf.append(keep.tile([P, HH, PACK], BF16, name="wa_bf1", tag="late", align_bytes=64))
         nc.vector.tensor_copy(*weave(wa_bf[1][:, 0:VEC_COLS, :], wa_raw[1][:, :, 0:VEC_COLS]))
         nc.scalar.copy(*weave(wa_bf[1][:, VEC_COLS:HH, :], wa_raw[1][:, :, VEC_COLS:HH]))
         nc.vector.quantize_mx(wa_q[1][:].bitcast(FP8X4), wa_s[1][:], wa_bf[1][:].rearrange("p c j -> p (c j)"))
+        w1s = keep.tile([P, PACK, P], U8, name="w1s", tag="late", align_bytes=64)
+        nc.gpsimd.tensor_copy(w1s[:], w1s_raw[:].rearrange("p (m t) -> p t m", t=PACK))
 
-        y = [keep.tile([P, H], F32, name=f"y{t}", align_bytes=64) for t in range(PACK)]
+        y = [stage.tile([P, H], F32, name=f"y{t}", offset=4 * H * t) for t in range(PACK)]
         for h in range(2):
             for t in range(PACK):
                 acc = psum.tile([P, HH], F32, name=f"acc{t}{h}", tag=f"bank{t}{h}")
@@ -97,51 +102,49 @@ def tile_picked_featglu_none_po_kernel(tc, x_words, x_scales, wa, gt, w1_words, 
                     acc[:], lhsT=xw[:, t, :].bitcast(FP8X4), lhsT_scale=xs[:, t, :],
                     rhs=wa_q[h][:].bitcast(FP8X4), rhs_scale=wa_s[h][:], start=True, stop=True,
                 )
-                if h == 1 and t > 0:
+                if (t >= 2 if h == 0 else t >= 1):
                     nc.vector.tensor_copy(y[t][:, h * HH : (h + 1) * HH], acc[:])
                 else:
                     nc.scalar.copy(y[t][:, h * HH : (h + 1) * HH], acc[:])
-
-        nc.vector.tensor_copy(w1s[:].rearrange("p t m -> p m t"), w1s_raw[:].rearrange("p (m t) -> p m t", t=PACK))
 
         out_v = out_0.rearrange("(p t) v -> p t v", t=PACK)
         words_v = out_1[0].rearrange("p n r -> p (n r)").bitcast(I32)
         o_q = keep.tile([P, V], U32, name="o_q", align_bytes=64)
         o_s = keep.tile([P, V], U8, name="o_s", align_bytes=64)
-        z_q, z_s = [], []
+        zf = keep.tile([P, PACK, V], F32, name="zf", align_bytes=64)
+        for t in range(PACK):
+            sg = keep.tile([P, V], F32, name=f"sg{t}", align_bytes=64)
+            nc.scalar.activation(sg[:], y[t][:].indirect(fb_t[:]), SIGMOID)
+            nc.vector.tensor_tensor(zf[:, t, :], y[t][:].indirect(fa_t[:]), sg[:], MULT)
+
+        zb = [keep.tile([P, VH, PACK], BF16, name=f"zb{g}", align_bytes=64) for g in range(2)]
+        zp = keep.tile([P, PACK, VH], BF16, name="zp", align_bytes=64)
+        zo, zi = weave(zb[0][:], zf[:, :, 0:VH])
+        nc.vector.tensor_tensor(
+            zo, zi, gate[:].rearrange("p (c t i) -> p c t i", c=1, i=1).to_broadcast([P, VH // PACK, PACK, PACK]), MULT
+        )
+        for t in range(PACK):
+            nc.scalar.activation(zp[:, t, :], zf[:, t, VH:V], COPY, scale=gate[:, t : t + 1])
+        nc.scalar.copy(*weave(zb[1][:], zp[:]))
+        z_q = [keep.tile([P, VH], U32, name=f"z_q{g}", align_bytes=64) for g in range(2)]
+        z_s = [keep.tile([P, VH], U8, name=f"z_s{g}", align_bytes=64) for g in range(2)]
         for g in range(2):
-            cols = slice(g * VH // 16, (g + 1) * VH // 16)
-            zf = keep.tile([P, PACK, VH], F32, name=f"zf{g}", align_bytes=64)
-            for t in range(PACK):
-                sg = keep.tile([P, VH], F32, name=f"sg{g}{t}", align_bytes=64)
-                nc.scalar.activation(sg[:], y[t][:].indirect(fb_t[:, cols]), SIGMOID)
-                nc.vector.tensor_tensor(zf[:, t, :], y[t][:].indirect(fa_t[:, cols]), sg[:], MULT)
-            zb = keep.tile([P, VH, PACK], BF16, name=f"zb{g}", align_bytes=64)
-            zo, zi = weave(zb[:], zf[:])
-            nc.vector.tensor_tensor(
-                zo, zi, gate[:].rearrange("p (c t i) -> p c t i", c=1, i=1).to_broadcast([P, VH // PACK, PACK, PACK]), MULT
-            )
-            z_q.append(keep.tile([P, VH], U32, name=f"z_q{g}", align_bytes=64))
-            z_s.append(keep.tile([P, VH], U8, name=f"z_s{g}", align_bytes=64))
-            nc.vector.quantize_mx(z_q[g][:].bitcast(FP8X4), z_s[g][:], zb[:].rearrange("p v t -> p (v t)"))
+            nc.vector.quantize_mx(z_q[g][:].bitcast(FP8X4), z_s[g][:], zb[g][:].rearrange("p v t -> p (v t)"))
 
         for g in range(2):
             vs = slice(g * VH, (g + 1) * VH)
-            acc = psum.tile([P, PACK, VH], F32, name=f"res{g}", tag=f"bank{g}0")
-            for t in range(PACK):
-                nc.tensor.matmul_mx(
-                    acc[:, t, :], lhsT=w1w[:, t, :].bitcast(FP4X4), lhsT_scale=w1s[:, t, :],
-                    rhs=z_q[g][:].bitcast(FP8X4), rhs_scale=z_s[g][:], start=True, stop=True,
-                )
             of = keep.tile([P, PACK, VH], F32, name=f"of{g}", align_bytes=64)
             ob = keep.tile([P, VH, PACK], BF16, name=f"ob{g}", align_bytes=64)
-            if g == 0:
-                nc.scalar.copy(of[:], acc[:])
-                nc.vector.tensor_copy(*weave(ob[:], of[:]))
-            else:
-                nc.vector.tensor_copy(ob[:], acc[:].rearrange("p t v -> p v t"))
-                nc.scalar.copy(of[:], acc[:])
+            for u in range(2):
+                acc = psum.tile([P, 2, VH], F32, name=f"res{g}{u}", tag=f"bank{2 * g + u}0")
+                for t in range(2 * u, 2 * u + 2):
+                    nc.tensor.matmul_mx(
+                        acc[:, t % 2, :], lhsT=w1w[:, t, :].bitcast(FP4X4), lhsT_scale=w1s[:, t, :],
+                        rhs=z_q[g][:].bitcast(FP8X4), rhs_scale=z_s[g][:], start=True, stop=True,
+                    )
+                nc.scalar.copy(of[:, 2 * u : 2 * u + 2, :], acc[:])
             nc.sync.dma_start(out_v[:, :, vs], of[:])
+            nc.vector.tensor_copy(*weave(ob[:], of[:]))
             nc.vector.quantize_mx(o_q[:, vs].bitcast(FP8X4), o_s[:, vs], ob[:].rearrange("p v t -> p (v t)"))
             nc.sync.dma_start(words_v[:, vs], o_q[:, vs].bitcast(I32))
         for q in range(4):

@@ -14,7 +14,6 @@ U8 = mybir.dt.uint8
 FP8X4 = mybir.dt.float8_e4m3fn_x4
 FP4X4 = mybir.dt.float4_e2m1fn_x4
 MULT = mybir.AluOpType.mult
-COPY = mybir.ActivationFunctionType.Copy
 SIGMOID = mybir.ActivationFunctionType.Sigmoid
 
 P = 128
@@ -36,12 +35,13 @@ def tile_picked_featglu_none_po_kernel(tc, x_words, x_scales, wa, gt, w1_words, 
     with ExitStack() as ctx:
         keep = ctx.enter_context(tc.tile_pool(name="keep", bufs=1))
         stage = ctx.enter_context(tc.tile_pool(name="stage", bufs=1))
+        late = ctx.enter_context(tc.tile_pool(name="late", bufs=1))
         psum = ctx.enter_context(tc.psum_pool(name="psum", bufs=1))
 
         offs_t = keep.tile([P, S // 16], U16, name="offs_t")
         fa_t = keep.tile([P, V // 16], U16, name="fa_t")
         fb_t = keep.tile([P, V // 16], U16, name="fb_t")
-        xw_all = keep.tile([P, T], I32, name="xw_all", tag="late", align_bytes=64)
+        xw_all = late.tile([P, T], I32, name="xw_all", align_bytes=64, offset=0)
         xs_all = keep.tile([P, T], U8, name="xs_all", tag="mid", align_bytes=64)
         wa_both = stage.tile([P, 2, PACK, HH], F32, name="wa_both", offset=0)
         wa_raw = [wa_both[:, h] for h in range(2)]
@@ -56,42 +56,42 @@ def tile_picked_featglu_none_po_kernel(tc, x_words, x_scales, wa, gt, w1_words, 
         nc.vector.memset(w1s_raw[:].bitcast(I32), 0)
 
         wa_v = wa.rearrange("(p j) c -> p j c", j=PACK)
-        nc.sync.dma_start(offs_t[:], offs)
-        nc.sync.dma_start(w1w_raw[:].bitcast(I32), w1_words[0].bitcast(I32))
         nc.sync.dma_start(wa_raw[0], wa_v[:, :, 0:HH])
+        nc.sync.dma_start(offs_t[:], offs)
+        nc.sync.dma_start(fb_t[:], fb)
         for q in range(4):
             nc.sync.dma_start(xs_all[32 * q : 32 * q + 4, :].bitcast(I32), x_scales[0][4 * q : 4 * q + 4, :].bitcast(I32))
         nc.sync.dma_start(xw_all[:], x_words[0].rearrange("p n r -> p (n r)").bitcast(I32))
         nc.sync.dma_start(wa_raw[1], wa_v[:, :, HH:H])
+        nc.sync.dma_start(w1w_raw[:].bitcast(I32), w1_words[0].bitcast(I32))
         for q in range(4):
             nc.sync.dma_start(w1s_raw[32 * q : 32 * q + 4, :].bitcast(I32), w1_scales[0][4 * q : 4 * q + 4, :].bitcast(I32))
-        nc.sync.dma_start(fb_t[:], fb)
         nc.sync.dma_start(fa_t[:], fa)
         nc.sync.dma_start(gate[:], gt.rearrange("(p t) o -> p (t o)", t=PACK))
         nc.scalar.activation(warm_out[:], warm_in[:], SIGMOID)
 
         wa_bf = [keep.tile([P, HH, PACK], BF16, name="wa_bf0", align_bytes=64)]
         wa_s = [keep.tile([P, HH], U8, name=f"wa_s{h}", align_bytes=64) for h in range(2)]
-        w1w = keep.tile([P, PACK, 2 * P], U8, name="w1w", align_bytes=64)
         xs_pick = keep.tile([P, S], U8, name="xs_pick", align_bytes=64)
         xs = keep.tile([P, PACK, P], U8, name="xs", align_bytes=64)
         xw = keep.tile([P, PACK, P], U32, name="xw", align_bytes=64)
 
         nc.scalar.copy(*weave(wa_bf[0][:], wa_raw[0]))
-        nc.vector.tensor_copy(
-            w1w[:].rearrange("p t (m b) -> p m t b", b=2), w1w_raw[:].rearrange("p (m t b) -> p m t b", t=PACK, b=2)
-        )
         nc.vector.tensor_copy(xs_pick[:], xs_all[:].indirect(offs_t[:]))
         wa_q = [keep.tile([P, HH], U32, name="wa_q0", tag="mid", align_bytes=64), keep.tile([P, HH], U32, name="wa_q1", align_bytes=64)]
         nc.vector.quantize_mx(wa_q[0][:].bitcast(FP8X4), wa_s[0][:], wa_bf[0][:].rearrange("p c j -> p (c j)"))
-        nc.vector.tensor_copy(xs[:].rearrange("p t m -> p m t"), xs_pick[:].rearrange("p (m t) -> p m t", t=PACK))
+        nc.vector.tensor_copy(xs[:], xs_pick[:].rearrange("p (m t) -> p t m", t=PACK))
         nc.vector.tensor_copy(xw[:].rearrange("p t m -> p m t"), xw_all[:].bitcast(U32).indirect(offs_t[:]))
 
-        wa_bf.append(keep.tile([P, HH, PACK], BF16, name="wa_bf1", tag="late", align_bytes=64))
+        wa_bf.append(late.tile([P, HH, PACK], BF16, name="wa_bf1", align_bytes=64, offset=0))
         nc.vector.tensor_copy(*weave(wa_bf[1][:, 0:VEC_COLS, :], wa_raw[1][:, :, 0:VEC_COLS]))
         nc.scalar.copy(*weave(wa_bf[1][:, VEC_COLS:HH, :], wa_raw[1][:, :, VEC_COLS:HH]))
         nc.vector.quantize_mx(wa_q[1][:].bitcast(FP8X4), wa_s[1][:], wa_bf[1][:].rearrange("p c j -> p (c j)"))
-        w1s = keep.tile([P, PACK, P], U8, name="w1s", tag="late", align_bytes=64)
+        w1w = late.tile([P, PACK, 2 * P], U8, name="w1w", align_bytes=64, offset=0)
+        w1s = late.tile([P, PACK, P], U8, name="w1s", align_bytes=64, offset=2 * N)
+        nc.vector.tensor_copy(
+            w1w[:].rearrange("p t (m b) -> p t m b", b=2), w1w_raw[:].rearrange("p (m t b) -> p t m b", t=PACK, b=2)
+        )
         nc.gpsimd.tensor_copy(w1s[:], w1s_raw[:].rearrange("p (m t) -> p t m", t=PACK))
 
         y = [stage.tile([P, H], F32, name=f"y{t}", offset=4 * H * t) for t in range(PACK)]
@@ -102,7 +102,7 @@ def tile_picked_featglu_none_po_kernel(tc, x_words, x_scales, wa, gt, w1_words, 
                     acc[:], lhsT=xw[:, t, :].bitcast(FP8X4), lhsT_scale=xs[:, t, :],
                     rhs=wa_q[h][:].bitcast(FP8X4), rhs_scale=wa_s[h][:], start=True, stop=True,
                 )
-                if (t >= 2 if h == 0 else t >= 1):
+                if h == 0 and t == PACK - 1:
                     nc.vector.tensor_copy(y[t][:, h * HH : (h + 1) * HH], acc[:])
                 else:
                     nc.scalar.copy(y[t][:, h * HH : (h + 1) * HH], acc[:])
@@ -111,21 +111,20 @@ def tile_picked_featglu_none_po_kernel(tc, x_words, x_scales, wa, gt, w1_words, 
         words_v = out_1[0].rearrange("p n r -> p (n r)").bitcast(I32)
         o_q = keep.tile([P, V], U32, name="o_q", align_bytes=64)
         o_s = keep.tile([P, V], U8, name="o_s", align_bytes=64)
-        zf = keep.tile([P, PACK, V], F32, name="zf", align_bytes=64)
+        zp = keep.tile([P, PACK, V], BF16, name="zp", align_bytes=64)
+        picked, gates = [], []
         for t in range(PACK):
-            sg = keep.tile([P, V], F32, name=f"sg{t}", align_bytes=64)
-            nc.scalar.activation(sg[:], y[t][:].indirect(fb_t[:]), SIGMOID)
-            nc.vector.tensor_tensor(zf[:, t, :], y[t][:].indirect(fa_t[:]), sg[:], MULT)
+            picked.append(keep.tile([P, V], F32, name=f"picked{t}", align_bytes=64))
+            gates.append(keep.tile([P, V], F32, name=f"sg{t}", align_bytes=64))
+            nc.scalar.activation(gates[t][:], y[t][:].indirect(fb_t[:]), SIGMOID)
+            nc.vector.tensor_copy(picked[t][:], y[t][:].indirect(fa_t[:]))
+        for t in range(PACK):
+            for vs in ([slice(0, V)] if t < PACK - 1 else [slice(0, VH), slice(VH, V)]):
+                nc.vector.scalar_tensor_tensor(zp[:, t, vs], picked[t][:, vs], gate[:, t : t + 1], gates[t][:, vs], MULT, MULT)
 
         zb = [keep.tile([P, VH, PACK], BF16, name=f"zb{g}", align_bytes=64) for g in range(2)]
-        zp = keep.tile([P, PACK, VH], BF16, name="zp", align_bytes=64)
-        zo, zi = weave(zb[0][:], zf[:, :, 0:VH])
-        nc.vector.tensor_tensor(
-            zo, zi, gate[:].rearrange("p (c t i) -> p c t i", c=1, i=1).to_broadcast([P, VH // PACK, PACK, PACK]), MULT
-        )
-        for t in range(PACK):
-            nc.scalar.activation(zp[:, t, :], zf[:, t, VH:V], COPY, scale=gate[:, t : t + 1])
-        nc.scalar.copy(*weave(zb[1][:], zp[:]))
+        nc.vector.tensor_copy(*weave(zb[0][:], zp[:, :, 0:VH]))
+        nc.vector.tensor_copy(*weave(zb[1][:], zp[:, :, VH:V]))
         z_q = [keep.tile([P, VH], U32, name=f"z_q{g}", align_bytes=64) for g in range(2)]
         z_s = [keep.tile([P, VH], U8, name=f"z_s{g}", align_bytes=64) for g in range(2)]
         for g in range(2):

from contextlib import ExitStack

import concourse.mybir as mybir

K, T, S, V, N, H = 512, 2048, 512, 256, 512, 512
FLOPS = 2 * S * K * H + 2 * N * S * V

F32 = mybir.dt.float32
BF16 = mybir.dt.bfloat16
I32 = mybir.dt.int32
U32 = mybir.dt.uint32
U16 = mybir.dt.uint16
U8 = mybir.dt.uint8
FP8X4 = mybir.dt.float8_e4m3fn_x4
FP4X4 = mybir.dt.float4_e2m1fn_x4
MULT = mybir.AluOpType.mult
SIGMOID = mybir.ActivationFunctionType.Sigmoid

P = 128
PACK = 4
HH = H // 2
VH = V // 2
VEC_COLS = 176


def weave(ap_out, ap_in):
    return (
        ap_out.rearrange("p (c i) t -> p c t i", i=PACK),
        ap_in.rearrange("p t (c i) -> p c t i", i=PACK),
    )


def tile_picked_featglu_none_po_kernel(tc, x_words, x_scales, wa, gt, w1_words, w1_scales, offs, fa, fb, out_0, out_1, out_2):
    nc = tc.nc
    with ExitStack() as ctx:
        keep = ctx.enter_context(tc.tile_pool(name="keep", bufs=1))
        stage = ctx.enter_context(tc.tile_pool(name="stage", bufs=1))
        late = ctx.enter_context(tc.tile_pool(name="late", bufs=1))
        psum = ctx.enter_context(tc.psum_pool(name="psum", bufs=1))

        offs_t = keep.tile([P, S // 16], U16, name="offs_t")
        fa_t = keep.tile([P, V // 16], U16, name="fa_t")
        fb_t = keep.tile([P, V // 16], U16, name="fb_t")
        xw_all = late.tile([P, T], I32, name="xw_all", align_bytes=64, offset=0)
        xs_all = keep.tile([P, T], U8, name="xs_all", tag="mid", align_bytes=64)
        wa_both = stage.tile([P, 2, PACK, HH], F32, name="wa_both", offset=0)
        wa_raw = [wa_both[:, h] for h in range(2)]
        gate = keep.tile([P, PACK], F32, name="gate")
        w1w_raw = keep.tile([P, 2 * N], U8, name="w1w_raw", align_bytes=64)
        w1s_raw = keep.tile([P, N], U8, name="w1s_raw", align_bytes=64)
        warm_in = keep.tile([P, 1], F32, name="warm_in")
        warm_out = keep.tile([P, 1], F32, name="warm_out")

        nc.vector.memset(xs_all[:].bitcast(I32), 0)
        nc.vector.memset(warm_in[:], 0.0)
        nc.vector.memset(w1s_raw[:].bitcast(I32), 0)

        wa_v = wa.rearrange("(p j) c -> p j c", j=PACK)
        nc.sync.dma_start(wa_raw[0], wa_v[:, :, 0:HH])
        nc.sync.dma_start(offs_t[:], offs)
        nc.sync.dma_start(fb_t[:], fb)
        for q in range(4):
            nc.sync.dma_start(xs_all[32 * q : 32 * q + 4, :].bitcast(I32), x_scales[0][4 * q : 4 * q + 4, :].bitcast(I32))
        nc.sync.dma_start(xw_all[:], x_words[0].rearrange("p n r -> p (n r)").bitcast(I32))
        nc.sync.dma_start(wa_raw[1], wa_v[:, :, HH:H])
        nc.sync.dma_start(w1w_raw[:].bitcast(I32), w1_words[0].bitcast(I32))
        for q in range(4):
            nc.sync.dma_start(w1s_raw[32 * q : 32 * q + 4, :].bitcast(I32), w1_scales[0][4 * q : 4 * q + 4, :].bitcast(I32))
        nc.sync.dma_start(fa_t[:], fa)
        nc.sync.dma_start(gate[:], gt.rearrange("(p t) o -> p (t o)", t=PACK))
        nc.scalar.activation(warm_out[:], warm_in[:], SIGMOID)

        wa_bf = [keep.tile([P, HH, PACK], BF16, name="wa_bf0", align_bytes=64)]
        wa_s = [keep.tile([P, HH], U8, name=f"wa_s{h}", align_bytes=64) for h in range(2)]
        xs_pick = keep.tile([P, S], U8, name="xs_pick", align_bytes=64)
        xs = keep.tile([P, PACK, P], U8, name="xs", align_bytes=64)
        xw = keep.tile([P, PACK, P], U32, name="xw", align_bytes=64)

        nc.scalar.copy(*weave(wa_bf[0][:], wa_raw[0]))
        nc.vector.tensor_copy(xs_pick[:], xs_all[:].indirect(offs_t[:]))
        wa_q = [keep.tile([P, HH], U32, name="wa_q0", tag="mid", align_bytes=64), keep.tile([P, HH], U32, name="wa_q1", align_bytes=64)]
        nc.vector.quantize_mx(wa_q[0][:].bitcast(FP8X4), wa_s[0][:], wa_bf[0][:].rearrange("p c j -> p (c j)"))
        nc.vector.tensor_copy(xs[:], xs_pick[:].rearrange("p (m t) -> p t m", t=PACK))
        nc.vector.tensor_copy(xw[:].rearrange("p t m -> p m t"), xw_all[:].bitcast(U32).indirect(offs_t[:]))

        wa_bf.append(late.tile([P, HH, PACK], BF16, name="wa_bf1", align_bytes=64, offset=0))
        nc.vector.tensor_copy(*weave(wa_bf[1][:, 0:VEC_COLS, :], wa_raw[1][:, :, 0:VEC_COLS]))
        nc.scalar.copy(*weave(wa_bf[1][:, VEC_COLS:HH, :], wa_raw[1][:, :, VEC_COLS:HH]))
        nc.vector.quantize_mx(wa_q[1][:].bitcast(FP8X4), wa_s[1][:], wa_bf[1][:].rearrange("p c j -> p (c j)"))
        w1w = late.tile([P, PACK, 2 * P], U8, name="w1w", align_bytes=64, offset=0)
        w1s = late.tile([P, PACK, P], U8, name="w1s", align_bytes=64, offset=2 * N)
        nc.vector.tensor_copy(
            w1w[:].rearrange("p t (m b) -> p t m b", b=2), w1w_raw[:].rearrange("p (m t b) -> p t m b", t=PACK, b=2)
        )
        nc.gpsimd.tensor_copy(w1s[:], w1s_raw[:].rearrange("p (m t) -> p t m", t=PACK))

        y = [stage.tile([P, H], F32, name=f"y{t}", offset=4 * H * t) for t in range(PACK)]
        for h in range(2):
            for t in range(PACK):
                acc = psum.tile([P, HH], F32, name=f"acc{t}{h}", tag=f"bank{t}{h}")
                nc.tensor.matmul_mx(
                    acc[:], lhsT=xw[:, t, :].bitcast(FP8X4), lhsT_scale=xs[:, t, :],
                    rhs=wa_q[h][:].bitcast(FP8X4), rhs_scale=wa_s[h][:], start=True, stop=True,
                )
                if h == 0 and t == PACK - 1:
                    nc.vector.tensor_copy(y[t][:, h * HH : (h + 1) * HH], acc[:])
                else:
                    nc.scalar.copy(y[t][:, h * HH : (h + 1) * HH], acc[:])

        out_v = out_0.rearrange("(p t) v -> p t v", t=PACK)
        words_v = out_1[0].rearrange("p n r -> p (n r)").bitcast(I32)
        o_q = keep.tile([P, V], U32, name="o_q", align_bytes=64)
        o_s = keep.tile([P, V], U8, name="o_s", align_bytes=64)
        zp = keep.tile([P, PACK, V], BF16, name="zp", align_bytes=64)
        picked, gates = [], []
        for t in range(PACK):
            picked.append(keep.tile([P, V], F32, name=f"picked{t}", align_bytes=64))
            gates.append(keep.tile([P, V], F32, name=f"sg{t}", align_bytes=64))
            nc.scalar.activation(gates[t][:], y[t][:].indirect(fb_t[:]), SIGMOID)
            nc.vector.tensor_copy(picked[t][:], y[t][:].indirect(fa_t[:]))
        for t in range(PACK):
            for vs in ([slice(0, V)] if t < PACK - 1 else [slice(0, VH), slice(VH, V)]):
                nc.vector.scalar_tensor_tensor(zp[:, t, vs], picked[t][:, vs], gate[:, t : t + 1], gates[t][:, vs], MULT, MULT)

        zb = [keep.tile([P, VH, PACK], BF16, name=f"zb{g}", align_bytes=64) for g in range(2)]
        nc.vector.tensor_copy(*weave(zb[0][:], zp[:, :, 0:VH]))
        nc.vector.tensor_copy(*weave(zb[1][:], zp[:, :, VH:V]))
        z_q = [keep.tile([P, VH], U32, name=f"z_q{g}", align_bytes=64) for g in range(2)]
        z_s = [keep.tile([P, VH], U8, name=f"z_s{g}", align_bytes=64) for g in range(2)]
        for g in range(2):
            nc.vector.quantize_mx(z_q[g][:].bitcast(FP8X4), z_s[g][:], zb[g][:].rearrange("p v t -> p (v t)"))

        for g in range(2):
            vs = slice(g * VH, (g + 1) * VH)
            of = keep.tile([P, PACK, VH], F32, name=f"of{g}", align_bytes=64)
            ob = keep.tile([P, VH, PACK], BF16, name=f"ob{g}", align_bytes=64)
            for u in range(2):
                acc = psum.tile([P, 2, VH], F32, name=f"res{g}{u}", tag=f"bank{2 * g + u}0")
                for t in range(2 * u, 2 * u + 2):
                    nc.tensor.matmul_mx(
                        acc[:, t % 2, :], lhsT=w1w[:, t, :].bitcast(FP4X4), lhsT_scale=w1s[:, t, :],
                        rhs=z_q[g][:].bitcast(FP8X4), rhs_scale=z_s[g][:], start=True, stop=True,
                    )
                nc.scalar.copy(of[:, 2 * u : 2 * u + 2, :], acc[:])
            nc.sync.dma_start(out_v[:, :, vs], of[:])
            nc.vector.tensor_copy(*weave(ob[:], of[:]))
            nc.vector.quantize_mx(o_q[:, vs].bitcast(FP8X4), o_s[:, vs], ob[:].rearrange("p v t -> p (v t)"))
            nc.sync.dma_start(words_v[:, vs], o_q[:, vs].bitcast(I32))
        for q in range(4):
            eng = nc.sync if q % 2 == 0 else nc.scalar
            eng.dma_start(out_2[0][4 * q : 4 * q + 4, :].bitcast(I32), o_s[32 * q : 32 * q + 4, :].bitcast(I32))
